import numpy as np, ml_dtypes
CORES = [26,28,98,100,106,108,122,124]
N = 8
import mx_ref
NC = 256
BF = ml_dtypes.bfloat16
def setup_inputs(rng):
    def f(*shape):
        return mx_ref.flush((rng.standard_normal(shape, dtype=np.float32) * np.exp2(rng.integers(-2, 3, shape[:-1] + (1,)))).astype(BF))
    return {"v": f(N, 128, 512), "p": f(N, 128, N * 4 * NC)}
def setup_inputs_blocks(rng):
    d = setup_inputs(rng)
    for k in ("v", "p"): d[k] = mx_ref.spread(d[k], rng, 2)
    return d
def setup_inputs_wide(rng):
    d = setup_inputs(rng)
    for k in ("v", "p"): d[k] = mx_ref.flush((d[k].astype(np.float32) * np.exp2(rng.integers(-8, 9, (N, 1, 1))).astype(np.float32)).astype(BF))
    return d
def setup_inputs_zeros(rng):
    d = setup_inputs(rng); v = d["p"].reshape(N, 128, -1, 4).copy()
    v[np.broadcast_to((rng.random((N, 1, v.shape[2], 1)) < 0.33), v.shape)] = 0
    d["p"] = v.reshape(d["p"].shape)
    return d
def reference(v, p):
    QV = [mx_ref.quantize(v[j]) for j in range(N)]
    y = np.zeros((N, 128, NC), np.float32)
    for r in range(N):
        for j in range(N):
            s = mx_ref.matmul(QV[j], mx_ref.quantize(p[r][:, 4 * NC * j:4 * NC * j + 4 * NC]))
            y[r] = s if j == 0 else y[r] + s
    return {"y": y}

@@ -1,0 +1,165 @@
+from concourse.bass import DstId, RemoteDMATransfer
+from concourse.mybir import dt
+
+N = 8
+NSIM = 128
+VW = 128
+PW = 256
+PRE = 2
+
+SCRATCH = {
+    "vb": ("sbuf", [128, 4 * VW], "bfloat16"),
+    "pb": ("sbuf", [128, N * 4 * PW], "bfloat16"),
+    "vq": ("sbuf", [128, N * VW], "float8_e4m3fn_x4"),
+    "vs": ("sbuf", [128, N * VW], "uint8"),
+    "pq": ("sbuf", [128, N * PW], "float8_e4m3fn_x4"),
+    "ps": ("sbuf", [128, N * PW], "uint8"),
+    "acc": ("psum", [128, 512], "float32"),
+    "yb": ("sbuf", [128, PW], "float32"),
+}
+SEMAPHORES = (["ldv", "qv", "gate", "hs", "hc", "sent", "mm", "yc", "st"]
+              + ["ldp%d" % i for i in range(N)] + ["qp%d" % j for j in range(N)] + ["a%d" % j for j in range(N)])
+
+
+def _bits(mask):
+    return bin(mask).count("1")
+
+
+def _match(flows, idle, cores, members, topo):
+    def options(flow):
+        srcs, y = flow
+        ok = [h for h in idle if all(topo.may_write(h, cores[d]) for d in members[y])]
+        return sorted(ok, key=lambda h: (topo.die(h) != topo.die(cores[srcs[0]]), h))
+    opts = [options(f) for f in flows]
+    todo = sorted(range(len(flows)), key=lambda i: len(opts[i]))
+    got = {}
+
+    def place(k):
+        if k == len(todo):
+            return True
+        for h in opts[todo[k]]:
+            if h not in got.values():
+                got[todo[k]] = h
+                if place(k + 1):
+                    return True
+                del got[todo[k]]
+        return False
+    return [got[i] for i in range(len(flows))] if place(0) else None
+
+
+def _plan(T, topo):
+    cores = list(T.cores)
+    chips = []
+    for c in cores:
+        if topo.chip(c) not in chips:
+            chips.append(topo.chip(c))
+    members = {x: [r for r in range(N) if topo.chip(cores[r]) == x] for x in chips}
+    jobs = []
+    for x in chips:
+        idle = [c for c in range(NSIM) if topo.chip(c) == x and c not in cores]
+        others = [y for y in chips if y != x]
+        flows = [([s], y) for s in members[x] for y in others]
+        helpers = _match(flows, idle, cores, members, topo)
+        if helpers is None:
+            flows = [(members[x], y) for y in others]
+            helpers = _match(flows, idle, cores, members, topo)
+        jobs += [(h, f[0], f[1]) for h, f in zip(helpers, flows)]
+    return cores, chips, members, jobs
+
+
+def _send(g, T, topo, me, lo, hi, dests, sem, codes):
+    mask = topo.mask(me, dests[0])
+    for d in dests:
+        mask &= topo.mask(me, d)
+    if codes:
+        ap = T.vq[:, VW * lo:VW * hi].bitcast(dt.uint8)
+    else:
+        ap = T.vs[:, VW * lo:VW * hi]
+    ids = [DstId(rid=topo.addr(d)[0], pnc=topo.addr(d)[1]) for d in dests]
+    g.remote_dma_fused([RemoteDMATransfer(dst_ids=ids, dma_engine_mask=mask, remote_sem=sem,
+                                          srcs=[ap], dsts=[ap for d in dests])], local_sem=T.sem.sent)
+    return _bits(mask)
+
+
+def _helper(g, core, T, topo, cores, members, job):
+    h, srcs, y = job
+    lo, hi = srcs[0], srcs[-1] + 1
+    dests = [cores[d] for d in members[y]]
+    due = sum(_bits(topo.mask(cores[s], core)) for s in srcs)
+    out = 0
+    g.wait_ge(T.sem.hs, due)
+    out += _send(g, T, topo, core, lo, hi, dests, T.sem["a%d" % lo], False)
+    g.wait_ge(T.sem.hc, due)
+    out += _send(g, T, topo, core, lo, hi, dests, T.sem["a%d" % lo], True)
+    g.wait_ge(T.sem.sent, out)
+
+
+def rank_program(g, core, T, topo):
+    cores, chips, members, jobs = _plan(T, topo)
+    rank = T.rank_of(core)
+    if rank is None:
+        for job in jobs:
+            if job[0] == core:
+                _helper(g, core, T, topo, cores, members, job)
+        return
+    mine = topo.chip(core)
+    sem = T.sem
+
+    def far(x):
+        hops = 1 if (topo.mates(x, mine) or topo.same_plane(x, mine)) else 2
+        lumped = max(len(j[1]) for j in jobs if j[1][0] in members[x])
+        return (hops, lumped, chips.index(x))
+    order = [mine] + sorted([x for x in chips if x != mine], key=far)
+
+    here = {rank: (sem.qv, 1)}
+    for s in members[mine]:
+        if s != rank:
+            here[s] = (sem["a%d" % s], 2 * _bits(topo.mask(cores[s], core)))
+    for h, srcs, y in jobs:
+        if y == mine:
+            n = _bits(topo.mask(h, cores[members[y][0]]))
+            for s in srcs:
+                here[s] = (sem["a%d" % srcs[0]], 2 * n)
+
+    g.sync.dma_start(T.vb[:], T.v[:]).then_inc(sem.ldv, 16)
+    for i, x in enumerate(order):
+        if i == PRE:
+            g.sync.wait_ge(sem.gate, 1)
+        lo, hi = members[x][0], members[x][-1] + 1
+        g.sync.dma_start(T.pb[:, 4 * PW * lo:4 * PW * hi], T.p[:, 4 * PW * lo:4 * PW * hi]).then_inc(sem["ldp%d" % i], 16)
+
+    slices = []
+    for x in order:
+        slices.append([rank] + [s for s in members[x] if s != rank] if x == mine else list(members[x]))
+    g.vector.wait_ge(sem.ldv, 16)
+    g.vector.quantize_mx(T.vq[:, VW * rank:VW * (rank + 1)], T.vs[:, VW * rank:VW * (rank + 1)], T.vb[:]).then_inc(sem.qv, 1)
+    for i, js in enumerate(slices):
+        g.vector.wait_ge(sem["ldp%d" % i], 16)
+        for j in js:
+            g.vector.quantize_mx(T.pq[:, PW * j:PW * (j + 1)], T.ps[:, PW * j:PW * (j + 1)],
+                                 T.pb[:, 4 * PW * j:4 * PW * (j + 1)]).then_inc(sem["qp%d" % j], 1)
+
+    helpers = [h for h, srcs, y in jobs if rank in srcs]
+    mates_here = [cores[s] for s in members[mine] if s != rank]
+    out = 0
+    g.wait_ge(sem.qv, 1)
+    out += _send(g, T, topo, core, rank, rank + 1, helpers, sem.hs, False)
+    out += _send(g, T, topo, core, rank, rank + 1, helpers, sem.hc, True)
+    out += _send(g, T, topo, core, rank, rank + 1, mates_here, sem["a%d" % rank], False)
+    out += _send(g, T, topo, core, rank, rank + 1, mates_here, sem["a%d" % rank], True)
+    g.sem_inc(sem.gate, 1)
+    g.wait_ge(sem.sent, out)
+
+    todo = [j for js in slices for j in js]
+    for k, j in enumerate(todo):
+        g.tensor.wait_ge(sem["qp%d" % j], 1)
+        g.tensor.wait_ge(here[j][0], here[j][1])
+        mm = g.tensor.matmul_mx(T.acc[:, 0:PW], T.vq[:, VW * j:VW * (j + 1)], T.vs[:, VW * j:VW * (j + 1)],
+                                T.pq[:, PW * j:PW * (j + 1)], T.ps[:, PW * j:PW * (j + 1)], k == 0, k == N - 1)
+    mm.then_inc(sem.mm, 1)
+
+    g.vector.wait_ge(sem.mm, 1)
+    g.vector.tensor_copy(T.yb[:], T.acc[:, 0:PW]).then_inc(sem.yc, 1)
+    g.sync.wait_ge(sem.yc, 1)
+    g.sync.dma_start(T.y[:], T.yb[:]).then_inc(sem.st, 16)
+    g.sync.wait_ge(sem.st, 16)

@@ -5,7 +5,9 @@ N = 8
 NSIM = 128
 VW = 128
 PW = 256
+CUT = (2, 2, 2, 2)
 PRE = 2
+HALVES = 2
 
 SCRATCH = {
     "vb": ("sbuf", [128, 4 * VW], "bfloat16"),
@@ -25,10 +27,19 @@ def _bits(mask):
     return bin(mask).count("1")
 
 
-def _match(flows, idle, cores, members, topo):
+def _part(mask, k, parts):
+    eng = [b for b in range(mask.bit_length()) if (mask >> b) & 1]
+    n = len(eng) // parts
+    out = 0
+    for b in eng[k * n:(k + 1) * n]:
+        out |= 1 << b
+    return out
+
+
+def _match(flows, idle, cores, topo):
     def options(flow):
-        srcs, y = flow
-        ok = [h for h in idle if all(topo.may_write(h, cores[d]) for d in members[y])]
+        srcs, dsts = flow
+        ok = [h for h in idle if all(topo.may_write(h, cores[d]) for d in dsts)]
         return sorted(ok, key=lambda h: (topo.die(h) != topo.die(cores[srcs[0]]), h))
     opts = [options(f) for f in flows]
     todo = sorted(range(len(flows)), key=lambda i: len(opts[i]))
@@ -58,19 +69,31 @@ def _plan(T, topo):
     for x in chips:
         idle = [c for c in range(NSIM) if topo.chip(c) == x and c not in cores]
         others = [y for y in chips if y != x]
-        flows = [([s], y) for s in members[x] for y in others]
-        helpers = _match(flows, idle, cores, members, topo)
+        flows = [([s], members[y]) for s in members[x] for y in others]
+        helpers = _match(flows, idle, cores, topo)
         if helpers is None:
-            flows = [(members[x], y) for y in others]
-            helpers = _match(flows, idle, cores, members, topo)
+            ok = [h for h in idle if all(topo.may_write(h, cores[d]) for y in others for d in members[y])][:len(others)]
+            ok.sort(key=lambda h: (sum(1 for k in ok if topo.die(k) == topo.die(h)), h))
+            ys = sorted(others, key=lambda y: (topo.mates(x, y), chips.index(y)))
+            seq = [members[y][i] for i in range(len(members[x])) for y in ys]
+            per = len(seq) // len(ok)
+            helpers = ok
+            flows = [(members[x], seq[k * per:(k + 1) * per]) for k in range(len(ok))]
         jobs += [(h, f[0], f[1]) for h, f in zip(helpers, flows)]
     return cores, chips, members, jobs
 
 
-def _send(g, T, topo, me, lo, hi, dests, sem, codes):
+def _mask(topo, me, dests, codes):
     mask = topo.mask(me, dests[0])
     for d in dests:
         mask &= topo.mask(me, d)
+    if all(topo.chip(d) == topo.chip(me) for d in dests):
+        return _part(mask, 1 if codes else 0, HALVES)
+    return mask
+
+
+def _send(g, T, topo, me, lo, hi, dests, sem, codes):
+    mask = _mask(topo, me, dests, codes)
     if codes:
         ap = T.vq[:, VW * lo:VW * hi].bitcast(dt.uint8)
     else:
@@ -81,15 +104,19 @@ def _send(g, T, topo, me, lo, hi, dests, sem, codes):
     return _bits(mask)
 
 
-def _helper(g, core, T, topo, cores, members, job):
-    h, srcs, y = job
+def _helper(g, core, T, topo, cores, jobs, job):
+    h, srcs, dsts = job
     lo, hi = srcs[0], srcs[-1] + 1
-    dests = [cores[d] for d in members[y]]
-    due = sum(_bits(topo.mask(cores[s], core)) for s in srcs)
+    dests = [cores[d] for d in dsts]
+    due = [0, 0]
+    for s in srcs:
+        to = [j[0] for j in jobs if s in j[1]]
+        due[0] += _bits(_mask(topo, cores[s], to, False))
+        due[1] += _bits(_mask(topo, cores[s], to, True))
     out = 0
-    g.wait_ge(T.sem.hs, due)
+    g.wait_ge(T.sem.hs, due[0])
     out += _send(g, T, topo, core, lo, hi, dests, T.sem["a%d" % lo], False)
-    g.wait_ge(T.sem.hc, due)
+    g.wait_ge(T.sem.hc, due[1])
     out += _send(g, T, topo, core, lo, hi, dests, T.sem["a%d" % lo], True)
     g.wait_ge(T.sem.sent, out)
 
@@ -100,7 +127,7 @@ def rank_program(g, core, T, topo):
     if rank is None:
         for job in jobs:
             if job[0] == core:
-                _helper(g, core, T, topo, cores, members, job)
+                _helper(g, core, T, topo, cores, jobs, job)
         return
     mine = topo.chip(core)
     sem = T.sem
@@ -110,36 +137,41 @@ def rank_program(g, core, T, topo):
         lumped = max(len(j[1]) for j in jobs if j[1][0] in members[x])
         return (hops, lumped, chips.index(x))
     order = [mine] + sorted([x for x in chips if x != mine], key=far)
+    todo = []
+    for x in order:
+        todo += [rank] + [s for s in members[x] if s != rank] if x == mine else list(members[x])
+    pieces = []
+    for n in CUT:
+        k = sum(len(q) for q in pieces)
+        pieces.append(todo[k:k + n])
+    gated = PRE < len(pieces)
 
     here = {rank: (sem.qv, 1)}
     for s in members[mine]:
         if s != rank:
-            here[s] = (sem["a%d" % s], 2 * _bits(topo.mask(cores[s], core)))
-    for h, srcs, y in jobs:
-        if y == mine:
-            n = _bits(topo.mask(h, cores[members[y][0]]))
+            here[s] = (sem["a%d" % s], _bits(_mask(topo, cores[s], [core], False)) + _bits(_mask(topo, cores[s], [core], True)))
+    for h, srcs, dsts in jobs:
+        if rank in dsts:
+            to = [cores[d] for d in dsts]
             for s in srcs:
-                here[s] = (sem["a%d" % srcs[0]], 2 * n)
+                here[s] = (sem["a%d" % srcs[0]], _bits(_mask(topo, h, to, False)) + _bits(_mask(topo, h, to, True)))
 
     g.sync.dma_start(T.vb[:], T.v[:]).then_inc(sem.ldv, 16)
-    for i, x in enumerate(order):
+    for i, js in enumerate(pieces):
         if i == PRE:
             g.sync.wait_ge(sem.gate, 1)
-        lo, hi = members[x][0], members[x][-1] + 1
+        lo, hi = min(js), max(js) + 1
         g.sync.dma_start(T.pb[:, 4 * PW * lo:4 * PW * hi], T.p[:, 4 * PW * lo:4 * PW * hi]).then_inc(sem["ldp%d" % i], 16)
 
-    slices = []
-    for x in order:
-        slices.append([rank] + [s for s in members[x] if s != rank] if x == mine else list(members[x]))
     g.vector.wait_ge(sem.ldv, 16)
     g.vector.quantize_mx(T.vq[:, VW * rank:VW * (rank + 1)], T.vs[:, VW * rank:VW * (rank + 1)], T.vb[:]).then_inc(sem.qv, 1)
-    for i, js in enumerate(slices):
+    for i, js in enumerate(pieces):
         g.vector.wait_ge(sem["ldp%d" % i], 16)
         for j in js:
             g.vector.quantize_mx(T.pq[:, PW * j:PW * (j + 1)], T.ps[:, PW * j:PW * (j + 1)],
                                  T.pb[:, 4 * PW * j:4 * PW * (j + 1)]).then_inc(sem["qp%d" % j], 1)
 
-    helpers = [h for h, srcs, y in jobs if rank in srcs]
+    helpers = [h for h, srcs, dsts in jobs if rank in srcs]
     mates_here = [cores[s] for s in members[mine] if s != rank]
     out = 0
     g.wait_ge(sem.qv, 1)
@@ -147,10 +179,10 @@ def rank_program(g, core, T, topo):
     out += _send(g, T, topo, core, rank, rank + 1, helpers, sem.hc, True)
     out += _send(g, T, topo, core, rank, rank + 1, mates_here, sem["a%d" % rank], False)
     out += _send(g, T, topo, core, rank, rank + 1, mates_here, sem["a%d" % rank], True)
-    g.sem_inc(sem.gate, 1)
+    if gated:
+        g.sem_inc(sem.gate, 1)
     g.wait_ge(sem.sent, out)
 
-    todo = [j for js in slices for j in js]
     for k, j in enumerate(todo):
         g.tensor.wait_ge(sem["qp%d" % j], 1)
         g.tensor.wait_ge(here[j][0], here[j][1])

@@ -7,7 +7,6 @@ VW = 128
 PW = 256
 CUT = (2, 2, 2, 2)
 PRE = 2
-HALVES = 2
 
 SCRATCH = {
     "vb": ("sbuf", [128, 4 * VW], "bfloat16"),
@@ -36,11 +35,14 @@ def _part(mask, k, parts):
     return out
 
 
-def _match(flows, idle, cores, topo):
+def _match(flows, pool, cores, topo):
     def options(flow):
         srcs, dsts = flow
-        ok = [h for h in idle if all(topo.may_write(h, cores[d]) for d in dsts)]
-        return sorted(ok, key=lambda h: (topo.die(h) != topo.die(cores[srcs[0]]), h))
+        home = topo.chip(cores[srcs[0]])
+        ok = [h for h in pool
+              if all(topo.may_write(h, cores[d]) for d in dsts) and all(topo.may_write(cores[s], h) for s in srcs)
+              and (topo.chip(h) == home or all(topo.mates(topo.chip(h), topo.chip(cores[d])) for d in dsts))]
+        return sorted(ok, key=lambda h: (topo.chip(h) != home, topo.die(h) != topo.die(cores[srcs[0]]), h))
     opts = [options(f) for f in flows]
     todo = sorted(range(len(flows)), key=lambda i: len(opts[i]))
     got = {}
@@ -67,33 +69,27 @@ def _plan(T, topo):
     members = {x: [r for r in range(N) if topo.chip(cores[r]) == x] for x in chips}
     jobs = []
     for x in chips:
-        idle = [c for c in range(NSIM) if topo.chip(c) == x and c not in cores]
         others = [y for y in chips if y != x]
+        pool = [c for c in range(NSIM) if c not in cores and (topo.chip(c) == x or (
+            topo.chip(c) not in chips and topo.same_plane(topo.chip(c), x)))]
+        pool = [c for c in pool if c not in [j[0] for j in jobs]]
         flows = [([s], members[y]) for s in members[x] for y in others]
-        helpers = _match(flows, idle, cores, topo)
-        if helpers is None:
-            ok = [h for h in idle if all(topo.may_write(h, cores[d]) for y in others for d in members[y])][:len(others)]
-            ok.sort(key=lambda h: (sum(1 for k in ok if topo.die(k) == topo.die(h)), h))
-            ys = sorted(others, key=lambda y: (topo.mates(x, y), chips.index(y)))
-            seq = [members[y][i] for i in range(len(members[x])) for y in ys]
-            per = len(seq) // len(ok)
-            helpers = ok
-            flows = [(members[x], seq[k * per:(k + 1) * per]) for k in range(len(ok))]
+        helpers = _match(flows, pool, cores, topo)
         jobs += [(h, f[0], f[1]) for h, f in zip(helpers, flows)]
     return cores, chips, members, jobs
 
 
-def _mask(topo, me, dests, codes):
+def _mask(topo, me, dests, half):
     mask = topo.mask(me, dests[0])
     for d in dests:
         mask &= topo.mask(me, d)
     if all(topo.chip(d) == topo.chip(me) for d in dests):
-        return _part(mask, 1 if codes else 0, HALVES)
+        return _part(mask, half, 2)
     return mask
 
 
-def _send(g, T, topo, me, lo, hi, dests, sem, codes):
-    mask = _mask(topo, me, dests, codes)
+def _send(g, T, topo, me, lo, hi, dests, sem, codes, half):
+    mask = _mask(topo, me, dests, half)
     if codes:
         ap = T.vq[:, VW * lo:VW * hi].bitcast(dt.uint8)
     else:
@@ -108,16 +104,14 @@ def _helper(g, core, T, topo, cores, jobs, job):
     h, srcs, dsts = job
     lo, hi = srcs[0], srcs[-1] + 1
     dests = [cores[d] for d in dsts]
-    due = [0, 0]
+    due = 0
     for s in srcs:
-        to = [j[0] for j in jobs if s in j[1]]
-        due[0] += _bits(_mask(topo, cores[s], to, False))
-        due[1] += _bits(_mask(topo, cores[s], to, True))
+        due += _bits(_mask(topo, cores[s], [j[0] for j in jobs if s in j[1]], 0))
     out = 0
-    g.wait_ge(T.sem.hs, due[0])
-    out += _send(g, T, topo, core, lo, hi, dests, T.sem["a%d" % lo], False)
-    g.wait_ge(T.sem.hc, due[1])
-    out += _send(g, T, topo, core, lo, hi, dests, T.sem["a%d" % lo], True)
+    g.wait_ge(T.sem.hs, due)
+    out += _send(g, T, topo, core, lo, hi, dests, T.sem["a%d" % lo], False, 0)
+    g.wait_ge(T.sem.hc, due)
+    out += _send(g, T, topo, core, lo, hi, dests, T.sem["a%d" % lo], True, 0)
     g.wait_ge(T.sem.sent, out)
 
 
@@ -134,8 +128,7 @@ def rank_program(g, core, T, topo):
 
     def far(x):
         hops = 1 if (topo.mates(x, mine) or topo.same_plane(x, mine)) else 2
-        lumped = max(len(j[1]) for j in jobs if j[1][0] in members[x])
-        return (hops, lumped, chips.index(x))
+        return (hops, chips.index(x))
     order = [mine] + sorted([x for x in chips if x != mine], key=far)
     todo = []
     for x in order:
@@ -149,12 +142,11 @@ def rank_program(g, core, T, topo):
     here = {rank: (sem.qv, 1)}
     for s in members[mine]:
         if s != rank:
-            here[s] = (sem["a%d" % s], _bits(_mask(topo, cores[s], [core], False)) + _bits(_mask(topo, cores[s], [core], True)))
+            here[s] = (sem["a%d" % s], 2 * _bits(_mask(topo, cores[s], [core], 0)))
     for h, srcs, dsts in jobs:
         if rank in dsts:
-            to = [cores[d] for d in dsts]
             for s in srcs:
-                here[s] = (sem["a%d" % srcs[0]], _bits(_mask(topo, h, to, False)) + _bits(_mask(topo, h, to, True)))
+                here[s] = (sem["a%d" % srcs[0]], 2 * _bits(_mask(topo, h, [cores[d] for d in dsts], 0)))
 
     g.sync.dma_start(T.vb[:], T.v[:]).then_inc(sem.ldv, 16)
     for i, js in enumerate(pieces):
@@ -175,10 +167,10 @@ def rank_program(g, core, T, topo):
     mates_here = [cores[s] for s in members[mine] if s != rank]
     out = 0
     g.wait_ge(sem.qv, 1)
-    out += _send(g, T, topo, core, rank, rank + 1, helpers, sem.hs, False)
-    out += _send(g, T, topo, core, rank, rank + 1, helpers, sem.hc, True)
-    out += _send(g, T, topo, core, rank, rank + 1, mates_here, sem["a%d" % rank], False)
-    out += _send(g, T, topo, core, rank, rank + 1, mates_here, sem["a%d" % rank], True)
+    out += _send(g, T, topo, core, rank, rank + 1, helpers, sem.hs, False, 0)
+    out += _send(g, T, topo, core, rank, rank + 1, helpers, sem.hc, True, 1)
+    out += _send(g, T, topo, core, rank, rank + 1, mates_here, sem["a%d" % rank], False, 0)
+    out += _send(g, T, topo, core, rank, rank + 1, mates_here, sem["a%d" % rank], True, 1)
     if gated:
         g.sem_inc(sem.gate, 1)
     g.wait_ge(sem.sent, out)

@@ -42,7 +42,11 @@ def _match(flows, pool, cores, topo):
         ok = [h for h in pool
               if all(topo.may_write(h, cores[d]) for d in dsts) and all(topo.may_write(cores[s], h) for s in srcs)
               and (topo.chip(h) == home or all(topo.mates(topo.chip(h), topo.chip(cores[d])) for d in dsts))]
-        return sorted(ok, key=lambda h: (topo.chip(h) != home, topo.die(h) != topo.die(cores[srcs[0]]), h))
+
+        def links(h):
+            return max(1 if (topo.mates(topo.chip(h), topo.chip(cores[d]))
+                             or topo.same_plane(topo.chip(h), topo.chip(cores[d]))) else 2 for d in dsts)
+        return sorted(ok, key=lambda h: (links(h), topo.chip(h) != home, topo.die(h) != topo.die(cores[srcs[0]]), h))
     opts = [options(f) for f in flows]
     todo = sorted(range(len(flows)), key=lambda i: len(opts[i]))
     got = {}

from concourse.bass import DstId, RemoteDMATransfer
from concourse.mybir import dt

N = 8
NSIM = 128
VW = 128
PW = 256
CUT = (2, 2, 2, 2)
PRE = 2

SCRATCH = {
    "vb": ("sbuf", [128, 4 * VW], "bfloat16"),
    "pb": ("sbuf", [128, N * 4 * PW], "bfloat16"),
    "vq": ("sbuf", [128, N * VW], "float8_e4m3fn_x4"),
    "vs": ("sbuf", [128, N * VW], "uint8"),
    "pq": ("sbuf", [128, N * PW], "float8_e4m3fn_x4"),
    "ps": ("sbuf", [128, N * PW], "uint8"),
    "acc": ("psum", [128, 512], "float32"),
    "yb": ("sbuf", [128, PW], "float32"),
}
SEMAPHORES = (["ldv", "qv", "gate", "hs", "hc", "sent", "mm", "yc", "st"]
              + ["ldp%d" % i for i in range(N)] + ["qp%d" % j for j in range(N)] + ["a%d" % j for j in range(N)])


def _bits(mask):
    return bin(mask).count("1")


def _part(mask, k, parts):
    eng = [b for b in range(mask.bit_length()) if (mask >> b) & 1]
    n = len(eng) // parts
    out = 0
    for b in eng[k * n:(k + 1) * n]:
        out |= 1 << b
    return out


def _match(flows, pool, cores, topo):
    def options(flow):
        srcs, dsts = flow
        home = topo.chip(cores[srcs[0]])
        ok = [h for h in pool
              if all(topo.may_write(h, cores[d]) for d in dsts) and all(topo.may_write(cores[s], h) for s in srcs)
              and (topo.chip(h) == home or all(topo.mates(topo.chip(h), topo.chip(cores[d])) for d in dsts))]

        def links(h):
            return max(1 if (topo.mates(topo.chip(h), topo.chip(cores[d]))
                             or topo.same_plane(topo.chip(h), topo.chip(cores[d]))) else 2 for d in dsts)
        return sorted(ok, key=lambda h: (links(h), topo.chip(h) != home, topo.die(h) != topo.die(cores[srcs[0]]), h))
    opts = [options(f) for f in flows]
    todo = sorted(range(len(flows)), key=lambda i: len(opts[i]))
    got = {}

    def place(k):
        if k == len(todo):
            return True
        for h in opts[todo[k]]:
            if h not in got.values():
                got[todo[k]] = h
                if place(k + 1):
                    return True
                del got[todo[k]]
        return False
    return [got[i] for i in range(len(flows))] if place(0) else None


def _plan(T, topo):
    cores = list(T.cores)
    chips = []
    for c in cores:
        if topo.chip(c) not in chips:
            chips.append(topo.chip(c))
    members = {x: [r for r in range(N) if topo.chip(cores[r]) == x] for x in chips}
    jobs = []
    for x in chips:
        others = [y for y in chips if y != x]
        pool = [c for c in range(NSIM) if c not in cores and (topo.chip(c) == x or (
            topo.chip(c) not in chips and topo.same_plane(topo.chip(c), x)))]
        pool = [c for c in pool if c not in [j[0] for j in jobs]]
        flows = [([s], members[y]) for s in members[x] for y in others]
        helpers = _match(flows, pool, cores, topo)
        jobs += [(h, f[0], f[1]) for h, f in zip(helpers, flows)]
    return cores, chips, members, jobs


def _mask(topo, me, dests, half):
    mask = topo.mask(me, dests[0])
    for d in dests:
        mask &= topo.mask(me, d)
    if all(topo.chip(d) == topo.chip(me) for d in dests):
        return _part(mask, half, 2)
    return mask


def _send(g, T, topo, me, lo, hi, dests, sem, codes, half):
    mask = _mask(topo, me, dests, half)
    if codes:
        ap = T.vq[:, VW * lo:VW * hi].bitcast(dt.uint8)
    else:
        ap = T.vs[:, VW * lo:VW * hi]
    ids = [DstId(rid=topo.addr(d)[0], pnc=topo.addr(d)[1]) for d in dests]
    g.remote_dma_fused([RemoteDMATransfer(dst_ids=ids, dma_engine_mask=mask, remote_sem=sem,
                                          srcs=[ap], dsts=[ap for d in dests])], local_sem=T.sem.sent)
    return _bits(mask)


def _helper(g, core, T, topo, cores, jobs, job):
    h, srcs, dsts = job
    lo, hi = srcs[0], srcs[-1] + 1
    dests = [cores[d] for d in dsts]
    due = 0
    for s in srcs:
        due += _bits(_mask(topo, cores[s], [j[0] for j in jobs if s in j[1]], 0))
    out = 0
    g.wait_ge(T.sem.hs, due)
    out += _send(g, T, topo, core, lo, hi, dests, T.sem["a%d" % lo], False, 0)
    g.wait_ge(T.sem.hc, due)
    out += _send(g, T, topo, core, lo, hi, dests, T.sem["a%d" % lo], True, 0)
    g.wait_ge(T.sem.sent, out)


def rank_program(g, core, T, topo):
    cores, chips, members, jobs = _plan(T, topo)
    rank = T.rank_of(core)
    if rank is None:
        for job in jobs:
            if job[0] == core:
                _helper(g, core, T, topo, cores, jobs, job)
        return
    mine = topo.chip(core)
    sem = T.sem

    def far(x):
        hops = 1 if (topo.mates(x, mine) or topo.same_plane(x, mine)) else 2
        return (hops, chips.index(x))
    order = [mine] + sorted([x for x in chips if x != mine], key=far)
    todo = []
    for x in order:
        todo += [rank] + [s for s in members[x] if s != rank] if x == mine else list(members[x])
    pieces = []
    for n in CUT:
        k = sum(len(q) for q in pieces)
        pieces.append(todo[k:k + n])
    gated = PRE < len(pieces)

    here = {rank: (sem.qv, 1)}
    for s in members[mine]:
        if s != rank:
            here[s] = (sem["a%d" % s], 2 * _bits(_mask(topo, cores[s], [core], 0)))
    for h, srcs, dsts in jobs:
        if rank in dsts:
            for s in srcs:
                here[s] = (sem["a%d" % srcs[0]], 2 * _bits(_mask(topo, h, [cores[d] for d in dsts], 0)))

    g.sync.dma_start(T.vb[:], T.v[:]).then_inc(sem.ldv, 16)
    for i, js in enumerate(pieces):
        if i == PRE:
            g.sync.wait_ge(sem.gate, 1)
        lo, hi = min(js), max(js) + 1
        g.sync.dma_start(T.pb[:, 4 * PW * lo:4 * PW * hi], T.p[:, 4 * PW * lo:4 * PW * hi]).then_inc(sem["ldp%d" % i], 16)

    g.vector.wait_ge(sem.ldv, 16)
    g.vector.quantize_mx(T.vq[:, VW * rank:VW * (rank + 1)], T.vs[:, VW * rank:VW * (rank + 1)], T.vb[:]).then_inc(sem.qv, 1)
    for i, js in enumerate(pieces):
        g.vector.wait_ge(sem["ldp%d" % i], 16)
        for j in js:
            g.vector.quantize_mx(T.pq[:, PW * j:PW * (j + 1)], T.ps[:, PW * j:PW * (j + 1)],
                                 T.pb[:, 4 * PW * j:4 * PW * (j + 1)]).then_inc(sem["qp%d" % j], 1)

    helpers = [h for h, srcs, dsts in jobs if rank in srcs]
    mates_here = [cores[s] for s in members[mine] if s != rank]
    out = 0
    g.wait_ge(sem.qv, 1)
    out += _send(g, T, topo, core, rank, rank + 1, helpers, sem.hs, False, 0)
    out += _send(g, T, topo, core, rank, rank + 1, helpers, sem.hc, True, 1)
    out += _send(g, T, topo, core, rank, rank + 1, mates_here, sem["a%d" % rank], False, 0)
    out += _send(g, T, topo, core, rank, rank + 1, mates_here, sem["a%d" % rank], True, 1)
    if gated:
        g.sem_inc(sem.gate, 1)
    g.wait_ge(sem.sent, out)

    for k, j in enumerate(todo):
        g.tensor.wait_ge(sem["qp%d" % j], 1)
        g.tensor.wait_ge(here[j][0], here[j][1])
        mm = g.tensor.matmul_mx(T.acc[:, 0:PW], T.vq[:, VW * j:VW * (j + 1)], T.vs[:, VW * j:VW * (j + 1)],
                                T.pq[:, PW * j:PW * (j + 1)], T.ps[:, PW * j:PW * (j + 1)], k == 0, k == N - 1)
    mm.then_inc(sem.mm, 1)

    g.vector.wait_ge(sem.mm, 1)
    g.vector.tensor_copy(T.yb[:], T.acc[:, 0:PW]).then_inc(sem.yc, 1)
    g.sync.wait_ge(sem.yc, 1)
    g.sync.dma_start(T.y[:], T.yb[:]).then_inc(sem.st, 16)
    g.sync.wait_ge(sem.st, 16)
